import numpy as np
import ml_dtypes


def mxq(x, axis, fmt="e4m3"):
    dtype, down = {"e4m3": (ml_dtypes.float8_e4m3fn, 7), "e5m2": (ml_dtypes.float8_e5m2, 14)}[fmt]
    v = np.moveaxis(np.asarray(x, np.float32).astype(ml_dtypes.bfloat16).astype(np.float64), axis, -1)
    blocks = v.reshape(v.shape[:-1] + (-1, 32))
    amax = np.abs(blocks).max(-1, keepdims=True)
    byte = np.maximum(np.where(amax > 0, np.frexp(amax)[1] - 1 + 127, 0) - down, 1)
    scale = np.exp2(byte - 127.0)
    codes = (blocks / scale).astype(np.float32).astype(dtype).astype(np.float64)
    return np.moveaxis((codes * scale).reshape(v.shape), -1, axis)


WIDE = False


def mx_kscale(k):
    if not WIDE:
        return np.ones(k)
    levels = np.array([30, -30])
    if k % 512:
        return np.exp2(np.random.permutation(np.resize(levels, k // 32))).repeat(32)
    a = np.empty((k // 512, 16))
    for p in range(k // 512):
        a[p, :8] = np.random.permutation(np.resize(levels, 8))
        for g in range(8):
            far = levels[np.abs(levels - a[p, g]) >= 10]
            a[p, g + 8] = far[np.random.randint(len(far))]
    return np.exp2(a.ravel()).repeat(32)


def f64(x):
    return np.asarray(x).astype(np.float64)


def striped(idx):
    return np.tile(idx.reshape(-1, 16).T, (8, 1)).astype(np.uint16)


def unstriped(offs):
    return offs[:16].T.reshape(-1).astype(np.int64)


E2M1 = np.array([0.0, 0.5, 1.0, 1.5, 2.0, 3.0, 4.0, 6.0, -0.0, -0.5, -1.0, -1.5, -2.0, -3.0, -4.0, -6.0])


def pack_weight(w, fmt):
    k, n = w.shape
    w = f64(np.asarray(w, np.float32).astype(ml_dtypes.bfloat16)).reshape(k // 32, 32, n)
    amax = np.abs(w).max(1)
    if fmt == "e4m3":
        byte = np.frexp(amax)[1] - 1 + 127 - 7
    else:
        mant, ex = np.frexp(amax / 6.0)
        byte = np.where(mant > 0.5, ex, ex - 1) + 127
    byte = np.clip(np.where(amax > 0, byte, 1), 1, 254)
    scaled = (w * np.exp2(127.0 - byte)[:, None, :]).reshape(k, n).astype(np.float32)
    by_word = np.ascontiguousarray(scaled.reshape(k // 512, 128, 4, n).transpose(0, 1, 3, 2))
    if fmt == "e4m3":
        words = by_word.astype(ml_dtypes.float8_e4m3fn).view(np.uint8)
    else:
        c = by_word.astype(ml_dtypes.float4_e2m1fn).view(np.uint8) & 0xF
        words = (c[..., 0::2] | (c[..., 1::2] << 4)).reshape(k // 512, 128, 2 * n)
    return np.ascontiguousarray(words), np.ascontiguousarray(byte.astype(np.uint8).reshape(k // 512, 16, n))


def unpack_weight(words, scales, fmt):
    g, _, n = scales.shape
    words = np.ascontiguousarray(words).reshape(g, 128, n, -1)
    if fmt == "e4m3":
        vals = words.view(ml_dtypes.float8_e4m3fn).astype(np.float64)
    else:
        nib = np.empty((g, 128, n, 4), np.uint8)
        nib[..., 0::2] = words & 0xF
        nib[..., 1::2] = words >> 4
        vals = E2M1[nib]
    vals = vals * np.repeat(np.exp2(scales.astype(np.float64) - 127.0), 8, axis=1)[..., None]
    return vals.transpose(0, 1, 3, 2).reshape(g * 512, n)


def sigmoid(v):
    return 1.0 / (1.0 + np.exp(-np.maximum(v, -700.0)))


def d_sigmoid(v):
    s = 1.0 / (1.0 + np.exp(-np.maximum(v, -700.0)))
    return s * (1.0 - s)


K, T, E, C, H, N = 128, 1024, 2, 512, 1024, 1024


def by_expert(wq, xq):
    return np.concatenate([wq[e].T @ xq[:, e * C:(e + 1) * C] for e in range(E)], axis=1)


def setup_inputs():
    n = np.random.standard_normal
    s = mx_kscale(N)[:, None]
    u = mx_kscale(H)
    w2 = [pack_weight(m, "e2m1") for m in n((E, N, H)) / np.sqrt(N) / s[None] * u[None, None, :]]
    w1 = [pack_weight(m, "e2m1") for m in n((E, H, K)) / np.sqrt(H) / u[None, :, None]]
    w3 = [pack_weight(m, "e2m1") for m in n((E, H, K)) / np.sqrt(H) / u[None, :, None]]
    return {
        "dyT": (n((N, T)) * s).astype(np.float32),
        "a1": n((H, E * C)).astype(np.float32),
        "a3": n((H, E * C)).astype(np.float32),
        "w2_words": np.stack([m[0] for m in w2]),
        "w2_scales": np.stack([m[1] for m in w2]),
        "w1_words": np.stack([m[0] for m in w1]),
        "w1_scales": np.stack([m[1] for m in w1]),
        "w3_words": np.stack([m[0] for m in w3]),
        "w3_scales": np.stack([m[1] for m in w3]),
        "gate": np.tile(np.random.uniform(0.2, 1.0, E * C), (N, 1)).astype(np.float32),
        "offs": striped(np.random.permutation(T)[:E * C]),
    }


def reference(dyT, a1, a3, w2_words, w2_scales, w1_words, w1_scales, w3_words, w3_scales, gate, offs):
    idx = unstriped(offs)
    w2 = np.stack([unpack_weight(w2_words[e], w2_scales[e], "e2m1") for e in range(E)])
    w1 = np.stack([unpack_weight(w1_words[e], w1_scales[e], "e2m1") for e in range(E)])
    w3 = np.stack([unpack_weight(w3_words[e], w3_scales[e], "e2m1") for e in range(E)])
    gq = mxq(f64(gate) * f64(dyT)[:, idx], 0, "e5m2")
    dh = by_expert(w2, gq)
    da1 = dh * f64(a3) * d_sigmoid(f64(a1))
    da3 = dh * sigmoid(f64(a1))
    dx = by_expert(w1, mxq(da1, 0, "e5m2")) + by_expert(w3, mxq(da3, 0, "e5m2"))
    out = np.zeros((K, T))
    out[:, idx] = dx
    return out

@@ -1,0 +1,207 @@
+from contextlib import ExitStack
+
+import concourse.mybir as mybir
+
+F32 = mybir.dt.float32
+BF16 = mybir.dt.bfloat16
+I32 = mybir.dt.int32
+U32 = mybir.dt.uint32
+U16 = mybir.dt.uint16
+U8 = mybir.dt.uint8
+E5M2X4 = mybir.dt.float8_e5m2_x4
+E2M1X4 = mybir.dt.float4_e2m1fn_x4
+ACT = mybir.ActivationFunctionType
+MULT = mybir.AluOpType.mult
+SUB = mybir.AluOpType.subtract
+
+P = 128
+PACK = 4
+PASS = P * PACK
+K, T, E, C, H, N = 128, 1024, 2, 512, 1024, 1024
+FLOPS = 2 * E * C * (N * H + 2 * H * K)
+
+
+def tile_moe_bdx_glu_sigmoid_kernel(
+    tc, dyT, a1, a3, w2_words, w2_scales, w1_words, w1_scales, w3_words, w3_scales, gate, offs, out
+):
+    nc = tc.nc
+    with ExitStack() as ctx:
+        keep = ctx.enter_context(tc.tile_pool(name="keep", bufs=1))
+        ring2 = ctx.enter_context(tc.tile_pool(name="ring2", bufs=2))
+        ring3 = ctx.enter_context(tc.tile_pool(name="ring3", bufs=3))
+        banks = ctx.enter_context(tc.psum_pool(name="banks", bufs=6))
+        sums = ctx.enter_context(tc.psum_pool(name="sums", bufs=1))
+
+        offsets = keep.tile([P, E * C // 16], U16, name="offsets")
+        gates = keep.tile([P, E * C], F32, name="gates")
+        dy = [keep.tile([P, T], F32, name=f"dy{b}") for b in range(N // P)]
+        w2_raw = [keep.tile([P, 2 * H], U8, name=f"w2_raw{b}", align_bytes=64) for b in range(4)]
+        w2_put = [keep.tile([P, 2 * H], U8, name=f"w2_put{b}", align_bytes=64) for b in range(4)]
+        w2s_raw = keep.tile([P, 4, H], U8, name="w2s_raw", align_bytes=64)
+        w2s_put = keep.tile([P, 4, H], U8, name="w2s_put", align_bytes=64)
+        w13 = [keep.tile([P, 4, 2 * K], U8, name=f"w13_{b}", align_bytes=64) for b in range(2)]
+        w13s = keep.tile([P, 2, 4, K], U8, name="w13s", align_bytes=64)
+        a1_t = [keep.tile([P, PACK, C], F32, name=f"a1_{b}") for b in range(4)]
+        a3_t = [keep.tile([P, PACK, C], F32, name=f"a3_{b}") for b in range(4)]
+        result = keep.tile([P, T], F32, name="result")
+
+        nc.gpsimd.memset(w2s_raw[:].rearrange("p b i -> p (b i)").bitcast(I32), 0)
+        nc.gpsimd.memset(w13s[:].rearrange("p w b k -> p (w b k)").bitcast(I32), 0)
+
+        for b in range(4):
+            nc.sync.dma_start(out=w2_raw[b][:].bitcast(I32), in_=w2_words[b // 2, b % 2].bitcast(I32))
+        nc.sync.dma_start(offsets[:], offs)
+        for e in range(E):
+            nc.sync.dma_start(out=gates[:, e * C:(e + 1) * C], in_=gate[0:P, e * C:(e + 1) * C])
+            if e == 0:
+                nc.sync.dma_start(out=dy[0][:], in_=dyT[0:PASS].rearrange("(p j) w -> p j w", j=PACK)[:, 0, :])
+        for b in range(1, 8):
+            s, j = divmod(b, PACK)
+            nc.sync.dma_start(out=dy[b][:], in_=dyT[s * PASS:(s + 1) * PASS].rearrange("(p j) w -> p j w", j=PACK)[:, j, :])
+        for q in range(4):
+            nc.scalar.dma_start(
+                out=w2s_raw[32 * q:32 * q + 4].rearrange("p b i -> p (b i)").bitcast(I32).rearrange("p (b i) -> p b i", b=4),
+                in_=w2_scales[:, :, 4 * q:4 * q + 4, :].bitcast(I32).rearrange("e s q i -> q (e s) i"),
+            )
+        for w, (words, scales) in enumerate(((w1_words, w1_scales), (w3_words, w3_scales))):
+            nc.scalar.dma_start(
+                out=w13[w][:].rearrange("p b i -> p (b i)").bitcast(I32).rearrange("p (b i) -> p b i", b=4),
+                in_=words.bitcast(I32).rearrange("e s p i -> p (e s) i"),
+            )
+            for q in range(4):
+                nc.scalar.dma_start(
+                    out=w13s[32 * q:32 * q + 4, w].rearrange("p b i -> p (b i)").bitcast(I32).rearrange("p (b i) -> p b i", b=4),
+                    in_=scales[:, :, 4 * q:4 * q + 4, :].bitcast(I32).rearrange("e s q i -> q (e s) i"),
+                )
+        for b in range(4):
+            e, h = divmod(b, 2)
+            for src, dst in ((a1, a1_t[b]), (a3, a3_t[b])):
+                nc.sync.dma_start(
+                    out=dst[:],
+                    in_=src[h * PASS:(h + 1) * PASS, e * C:(e + 1) * C].rearrange("(p j) c -> p j c", j=PACK),
+                )
+
+        for b in range(4):
+            nc.vector.tensor_copy(
+                out=w2_put[b][:].bitcast(U16).rearrange("p (h t m) -> p h t m", h=2, t=PACK),
+                in_=w2_raw[b][:].bitcast(U16).rearrange("p (h m t) -> p h t m", h=2, t=PACK),
+            )
+        for b in range(4):
+            nc.vector.tensor_copy(
+                out=w2s_put[:, b].rearrange("p (h t m) -> p h t m", h=2, t=PACK),
+                in_=w2s_raw[:, b].rearrange("p (h m t) -> p h t m", h=2, t=PACK),
+            )
+
+        g_codes, g_scales = {}, {}
+
+        def gather(e, s, j, g4):
+            nc.vector.tensor_tensor(
+                out=g4[:, j, :],
+                in0=dy[s * PACK + j][:].indirect(offsets[:, e * C // 16:(e + 1) * C // 16]),
+                in1=gates[:, e * C:(e + 1) * C],
+                op=MULT,
+            )
+
+        def interleaved(dst):
+            return dst[:].rearrange("p (c i) t -> p c t i", i=4)
+
+        def planes(src):
+            return src[:].rearrange("p t (c i) -> p c t i", i=4)
+
+        def quantise(src, name):
+            codes = keep.tile([P, C], U32, name=name + "_codes", align_bytes=64)
+            scales = keep.tile([P, C], U8, name=name + "_scales", align_bytes=64)
+            nc.vector.quantize_mx(
+                out=codes[:].bitcast(E5M2X4), scales=scales[:], in_=src[:].rearrange("p c t -> p (c t)")
+            )
+            return codes, scales
+
+        def finish_g(e, s, g4):
+            gb = ring2.tile([P, C, PACK], BF16, name="gb", align_bytes=64)
+            nc.scalar.copy(out=interleaved(gb), in_=planes(g4))
+            g_codes[e, s], g_scales[e, s] = quantise(gb, f"g{e}{s}")
+
+        g4s = [ring3.tile([P, PACK, C], F32, name="g4") for e in range(E)]
+        for j in range(PACK):
+            for e in range(E):
+                gather(e, 0, j, g4s[e])
+        for e in range(E):
+            finish_g(e, 0, g4s[e])
+        for e in range(E):
+            g4 = ring3.tile([P, PACK, C], F32, name="g4")
+            for j in range(PACK):
+                gather(e, 1, j, g4)
+            finish_g(e, 1, g4)
+
+        dx = [sums.tile([P, C], F32, name=f"dx{e}") for e in range(E)]
+        held = {}
+
+        def saved(b):
+            s = a1_t[b]
+            nc.scalar.activation(out=s[:], in_=s[:], func=ACT.Sigmoid)
+            v = a3_t[b]
+            nc.vector.scalar_tensor_tensor(out=v[:], in0=s[:], scalar=1.0, in1=v[:], op0=SUB, op1=MULT)
+
+        def first_products(b):
+            e, h = divmod(b, 2)
+            u = ring2.tile([P, PACK, C], F32, name="u")
+            for t in range(PACK):
+                dh = banks.tile([P, C], F32, name="dh")
+                col = h * PASS + t * P
+                for s in range(2):
+                    nc.tensor.matmul_mx(
+                        out=dh[:],
+                        lhsT=w2_put[2 * e + s][:, 2 * col:2 * (col + P)].bitcast(E2M1X4),
+                        lhsT_scale=w2s_put[:, 2 * e + s, col:col + P],
+                        rhs=g_codes[e, s][:].bitcast(E5M2X4),
+                        rhs_scale=g_scales[e, s][:],
+                        start=(s == 0),
+                        stop=(s == 1),
+                    )
+                nc.vector.tensor_tensor(out=u[:, t, :], in0=dh[:], in1=a1_t[b][:, t, :], op=MULT)
+            held[b] = u
+
+        def gradients(b):
+            u = held[b]
+            d3 = ring2.tile([P, C, PACK], BF16, name="d3", align_bytes=64)
+            nc.scalar.activation(out=interleaved(d3), in_=planes(u), func=ACT.Copy, scale=-1.0)
+            d1 = ring2.tile([P, C, PACK], BF16, name="d1", align_bytes=64)
+            nc.vector.tensor_tensor(out=interleaved(d1), in0=planes(u), in1=planes(a3_t[b]), op=MULT)
+            held[b] = (d1, d3)
+
+        def second_products(b):
+            e, h = divmod(b, 2)
+            d1, d3 = held[b]
+            for w, src in ((0, d1), (1, d3)):
+                codes, scales = quantise(src, f"d{w}_{b}")
+                nc.tensor.matmul_mx(
+                    out=dx[e][:],
+                    lhsT=w13[w][:, b, :].bitcast(E2M1X4),
+                    lhsT_scale=w13s[:, w, b, :],
+                    rhs=codes[:].bitcast(E5M2X4),
+                    rhs_scale=scales[:],
+                    start=(h == 0 and w == 0),
+                    stop=(h == 1 and w == 1),
+                )
+
+        def finish(e):
+            dx_sb = ring2.tile([P, C], F32, name="dx_sb")
+            nc.scalar.activation(out=dx_sb[:], in_=dx[e][:], func=ACT.Copy, scale=-1.0)
+            return dx_sb
+
+        def scatter(e, dx_sb):
+            nc.vector.tensor_copy(result[:].indirect(offsets[:, e * C // 16:(e + 1) * C // 16]), dx_sb[:])
+
+        saved(0)
+        first_products(0)
+        for b in range(4):
+            gradients(b)
+            if b < 3:
+                saved(b + 1)
+                first_products(b + 1)
+            second_products(b)
+            if b == 1:
+                dx_sb0 = finish(0)
+        scatter(0, dx_sb0)
+        scatter(1, finish(1))
+        nc.sync.dma_start(out=out, in_=result[:])

@@ -28,40 +28,48 @@ def tile_moe_bdx_glu_sigmoid_kernel(
     with ExitStack() as ctx:
         keep = ctx.enter_context(tc.tile_pool(name="keep", bufs=1))
         ring2 = ctx.enter_context(tc.tile_pool(name="ring2", bufs=2))
-        ring3 = ctx.enter_context(tc.tile_pool(name="ring3", bufs=3))
         banks = ctx.enter_context(tc.psum_pool(name="banks", bufs=6))
         sums = ctx.enter_context(tc.psum_pool(name="sums", bufs=1))
 
         offsets = keep.tile([P, E * C // 16], U16, name="offsets")
         gates = keep.tile([P, E * C], F32, name="gates")
-        dy = [keep.tile([P, T], F32, name=f"dy{b}") for b in range(N // P)]
+        dy = [keep.tile([P, T + 8], F32, name=f"dy{b}") for b in range(N // P)]
         w2_raw = [keep.tile([P, 2 * H], U8, name=f"w2_raw{b}", align_bytes=64) for b in range(4)]
         w2_put = [keep.tile([P, 2 * H], U8, name=f"w2_put{b}", align_bytes=64) for b in range(4)]
-        w2s_raw = keep.tile([P, 4, H], U8, name="w2s_raw", align_bytes=64)
-        w2s_put = keep.tile([P, 4, H], U8, name="w2s_put", align_bytes=64)
+        w2s_raw = keep.tile([P, H], U8, name="w2s_raw", align_bytes=64)
+        w2s_put = [keep.tile([P, H], U8, name=f"w2s_put{b}", align_bytes=64) for b in range(4)]
         w13 = [keep.tile([P, 4, 2 * K], U8, name=f"w13_{b}", align_bytes=64) for b in range(2)]
         w13s = keep.tile([P, 2, 4, K], U8, name="w13s", align_bytes=64)
         a1_t = [keep.tile([P, PACK, C], F32, name=f"a1_{b}") for b in range(4)]
         a3_t = [keep.tile([P, PACK, C], F32, name=f"a3_{b}") for b in range(4)]
         result = keep.tile([P, T], F32, name="result")
 
-        nc.gpsimd.memset(w2s_raw[:].rearrange("p b i -> p (b i)").bitcast(I32), 0)
+        nc.gpsimd.memset(w2s_raw[:].bitcast(I32), 0)
+        for b in range(8):
+            nc.gpsimd.memset(dy[b][:, T:], 0.0)
+        for b in range(1, 4):
+            nc.gpsimd.memset(w2s_put[b][:].bitcast(I32), 0)
         nc.gpsimd.memset(w13s[:].rearrange("p w b k -> p (w b k)").bitcast(I32), 0)
 
-        for b in range(4):
+        def load_w2(b):
             nc.sync.dma_start(out=w2_raw[b][:].bitcast(I32), in_=w2_words[b // 2, b % 2].bitcast(I32))
+
+        def load_dy(b):
+            s, j = divmod(b, PACK)
+            nc.sync.dma_start(out=dy[b][:, 0:T], in_=dyT[s * PASS:(s + 1) * PASS].rearrange("(p j) w -> p j w", j=PACK)[:, j, :])
+
+        for b in range(4):
+            load_w2(b)
         nc.sync.dma_start(offsets[:], offs)
         for e in range(E):
             nc.sync.dma_start(out=gates[:, e * C:(e + 1) * C], in_=gate[0:P, e * C:(e + 1) * C])
-            if e == 0:
-                nc.sync.dma_start(out=dy[0][:], in_=dyT[0:PASS].rearrange("(p j) w -> p j w", j=PACK)[:, 0, :])
-        for b in range(1, 8):
-            s, j = divmod(b, PACK)
-            nc.sync.dma_start(out=dy[b][:], in_=dyT[s * PASS:(s + 1) * PASS].rearrange("(p j) w -> p j w", j=PACK)[:, j, :])
+            load_dy(e)
+        for b in range(2, 8):
+            load_dy(b)
         for q in range(4):
             nc.scalar.dma_start(
-                out=w2s_raw[32 * q:32 * q + 4].rearrange("p b i -> p (b i)").bitcast(I32).rearrange("p (b i) -> p b i", b=4),
-                in_=w2_scales[:, :, 4 * q:4 * q + 4, :].bitcast(I32).rearrange("e s q i -> q (e s) i"),
+                out=w2s_raw[32 * q:32 * q + 16, :].bitcast(I32),
+                in_=w2_scales[:, :, 4 * q:4 * q + 4, :].bitcast(I32).rearrange("e s q i -> (e s) q i"),
             )
         for w, (words, scales) in enumerate(((w1_words, w1_scales), (w3_words, w3_scales))):
             nc.scalar.dma_start(
@@ -86,52 +94,58 @@ def tile_moe_bdx_glu_sigmoid_kernel(
                 out=w2_put[b][:].bitcast(U16).rearrange("p (h t m) -> p h t m", h=2, t=PACK),
                 in_=w2_raw[b][:].bitcast(U16).rearrange("p (h m t) -> p h t m", h=2, t=PACK),
             )
-        for b in range(4):
-            nc.vector.tensor_copy(
-                out=w2s_put[:, b].rearrange("p (h t m) -> p h t m", h=2, t=PACK),
-                in_=w2s_raw[:, b].rearrange("p (h m t) -> p h t m", h=2, t=PACK),
-            )
+        nc.vector.tensor_copy(
+            out=w2s_put[0][:].rearrange("p (h t m) -> p h t m", h=2, t=PACK),
+            in_=w2s_raw[:].rearrange("p (h m t) -> p h t m", h=2, t=PACK),
+        )
+        for b in range(1, 4):
+            for q in range(4):
+                nc.scalar.dma_start(
+                    out=w2s_put[b][32 * q:32 * q + 4, :].bitcast(I32),
+                    in_=w2s_put[0][32 * q + 4 * b:32 * q + 4 * b + 4, :].bitcast(I32),
+                )
 
         g_codes, g_scales = {}, {}
 
-        def gather(e, s, j, g4):
+        def gather(s, j, g4, first, last):
+            slots = slice(first * C, last * C)
             nc.vector.tensor_tensor(
-                out=g4[:, j, :],
-                in0=dy[s * PACK + j][:].indirect(offsets[:, e * C // 16:(e + 1) * C // 16]),
-                in1=gates[:, e * C:(e + 1) * C],
+                out=g4[:, j, slots],
+                in0=dy[s * PACK + j][:].indirect(offsets[:, first * C // 16:last * C // 16]),
+                in1=gates[:, slots],
                 op=MULT,
             )
 
         def interleaved(dst):
-            return dst[:].rearrange("p (c i) t -> p c t i", i=4)
+            return dst.rearrange("p (c i) t -> p c t i", i=4)
 
         def planes(src):
-            return src[:].rearrange("p t (c i) -> p c t i", i=4)
+            return src.rearrange("p t (c i) -> p c t i", i=4)
 
         def quantise(src, name):
             codes = keep.tile([P, C], U32, name=name + "_codes", align_bytes=64)
             scales = keep.tile([P, C], U8, name=name + "_scales", align_bytes=64)
             nc.vector.quantize_mx(
-                out=codes[:].bitcast(E5M2X4), scales=scales[:], in_=src[:].rearrange("p c t -> p (c t)")
+                out=codes[:].bitcast(E5M2X4), scales=scales[:], in_=src.rearrange("p c t -> p (c t)")
             )
             return codes, scales
 
         def finish_g(e, s, g4):
             gb = ring2.tile([P, C, PACK], BF16, name="gb", align_bytes=64)
-            nc.scalar.copy(out=interleaved(gb), in_=planes(g4))
-            g_codes[e, s], g_scales[e, s] = quantise(gb, f"g{e}{s}")
+            nc.scalar.copy(out=interleaved(gb[:]), in_=planes(g4[:, :, e * C:(e + 1) * C]))
+            g_codes[e, s], g_scales[e, s] = quantise(gb[:], f"g{e}{s}")
 
-        g4s = [ring3.tile([P, PACK, C], F32, name="g4") for e in range(E)]
-        for j in range(PACK):
-            for e in range(E):
-                gather(e, 0, j, g4s[e])
+        g4 = [ring2.tile([P, PACK, E * C], F32, name="g4") for s in range(2)]
+        gather(0, 0, g4[0], 0, 1)
+        gather(0, 0, g4[0], 1, 2)
+        for j in range(1, PACK):
+            gather(0, j, g4[0], 0, E)
         for e in range(E):
-            finish_g(e, 0, g4s[e])
+            finish_g(e, 0, g4[0])
         for e in range(E):
-            g4 = ring3.tile([P, PACK, C], F32, name="g4")
             for j in range(PACK):
-                gather(e, 1, j, g4)
-            finish_g(e, 1, g4)
+                gather(1, j, g4[1], e, e + 1)
+            finish_g(e, 1, g4[1])
 
         dx = [sums.tile([P, C], F32, name=f"dx{e}") for e in range(E)]
         held = {}
@@ -152,7 +166,7 @@ def tile_moe_bdx_glu_sigmoid_kernel(
                     nc.tensor.matmul_mx(
                         out=dh[:],
                         lhsT=w2_put[2 * e + s][:, 2 * col:2 * (col + P)].bitcast(E2M1X4),
-                        lhsT_scale=w2s_put[:, 2 * e + s, col:col + P],
+                        lhsT_scale=w2s_put[2 * e + s][:, col:col + P],
                         rhs=g_codes[e, s][:].bitcast(E5M2X4),
                         rhs_scale=g_scales[e, s][:],
                         start=(s == 0),
@@ -163,17 +177,15 @@ def tile_moe_bdx_glu_sigmoid_kernel(
 
         def gradients(b):
             u = held[b]
-            d3 = ring2.tile([P, C, PACK], BF16, name="d3", align_bytes=64)
-            nc.scalar.activation(out=interleaved(d3), in_=planes(u), func=ACT.Copy, scale=-1.0)
-            d1 = ring2.tile([P, C, PACK], BF16, name="d1", align_bytes=64)
-            nc.vector.tensor_tensor(out=interleaved(d1), in0=planes(u), in1=planes(a3_t[b]), op=MULT)
-            held[b] = (d1, d3)
+            d = ring2.tile([P, 2, C, PACK], BF16, name="d", align_bytes=64)
+            nc.scalar.activation(out=interleaved(d[:, 1]), in_=planes(u[:]), func=ACT.Copy, scale=-1.0)
+            nc.vector.tensor_tensor(out=interleaved(d[:, 0]), in0=planes(u[:]), in1=planes(a3_t[b][:]), op=MULT)
+            held[b] = d
 
         def second_products(b):
             e, h = divmod(b, 2)
-            d1, d3 = held[b]
-            for w, src in ((0, d1), (1, d3)):
-                codes, scales = quantise(src, f"d{w}_{b}")
+            for w in range(2):
+                codes, scales = quantise(held[b][:, w], f"d{w}_{b}")
                 nc.tensor.matmul_mx(
                     out=dx[e][:],
                     lhsT=w13[w][:, b, :].bitcast(E2M1X4),
@@ -184,13 +196,11 @@ def tile_moe_bdx_glu_sigmoid_kernel(
                     stop=(h == 1 and w == 1),
                 )
 
-        def finish(e):
-            dx_sb = ring2.tile([P, C], F32, name="dx_sb")
-            nc.scalar.activation(out=dx_sb[:], in_=dx[e][:], func=ACT.Copy, scale=-1.0)
-            return dx_sb
+        def finish(e, dx_sb):
+            nc.scalar.activation(out=dx_sb[:, 0, :], in_=dx[e][:], func=ACT.Copy, scale=-1.0)
 
         def scatter(e, dx_sb):
-            nc.vector.tensor_copy(result[:].indirect(offsets[:, e * C // 16:(e + 1) * C // 16]), dx_sb[:])
+            nc.vector.tensor_copy(result[:].indirect(offsets[:, e * C // 16:(e + 1) * C // 16]), dx_sb[:, 0, :])
 
         saved(0)
         first_products(0)
@@ -200,8 +210,8 @@ def tile_moe_bdx_glu_sigmoid_kernel(
                 saved(b + 1)
                 first_products(b + 1)
             second_products(b)
-            if b == 1:
-                dx_sb0 = finish(0)
-        scatter(0, dx_sb0)
-        scatter(1, finish(1))
+        landing = [ring2.tile([P, PACK, C], F32, name="u") for z in range(2)]
+        for e in range(E):
+            finish(e, landing[1 - e])
+            scatter(e, landing[1 - e])
         nc.sync.dma_start(out=out, in_=result[:])

@@ -175,17 +175,27 @@ def tile_moe_bdx_glu_sigmoid_kernel(
                 nc.vector.tensor_tensor(out=u[:, t, :], in0=dh[:], in1=a1_t[b][:, t, :], op=MULT)
             held[b] = u
 
-        def gradients(b):
+        def product(engine, b, first, last):
+            u, d = held[b]
+            engine.tensor_tensor(
+                out=interleaved(d[:, 0, first:last, :]),
+                in0=planes(u[:, :, first:last]),
+                in1=planes(a3_t[b][:, :, first:last]),
+                op=MULT,
+            )
+
+        def gradients(b, share):
             u = held[b]
             d = ring2.tile([P, 2, C, PACK], BF16, name="d", align_bytes=64)
+            held[b] = (u, d)
+            for first in range(0, share, 128):
+                product(nc.gpsimd, b, first, first + 128)
             nc.scalar.activation(out=interleaved(d[:, 1]), in_=planes(u[:]), func=ACT.Copy, scale=-1.0)
-            nc.vector.tensor_tensor(out=interleaved(d[:, 0]), in0=planes(u[:]), in1=planes(a3_t[b][:]), op=MULT)
-            held[b] = d
 
         def second_products(b):
             e, h = divmod(b, 2)
             for w in range(2):
-                codes, scales = quantise(held[b][:, w], f"d{w}_{b}")
+                codes, scales = quantise(held[b][1][:, w], f"d{w}_{b}")
                 nc.tensor.matmul_mx(
                     out=dx[e][:],
                     lhsT=w13[w][:, b, :].bitcast(E2M1X4),
@@ -204,11 +214,15 @@ def tile_moe_bdx_glu_sigmoid_kernel(
 
         saved(0)
         first_products(0)
+        saved(1)
         for b in range(4):
-            gradients(b)
+            share = 256 if b < 3 else 0
+            gradients(b, share)
             if b < 3:
-                saved(b + 1)
                 first_products(b + 1)
+            product(nc.vector, b, share, C)
+            if b < 2:
+                saved(b + 2)
             second_products(b)
         landing = [ring2.tile([P, PACK, C], F32, name="u") for z in range(2)]
         for e in range(E):

from contextlib import ExitStack

import concourse.mybir as mybir

F32 = mybir.dt.float32
BF16 = mybir.dt.bfloat16
I32 = mybir.dt.int32
U32 = mybir.dt.uint32
U16 = mybir.dt.uint16
U8 = mybir.dt.uint8
E5M2X4 = mybir.dt.float8_e5m2_x4
E2M1X4 = mybir.dt.float4_e2m1fn_x4
ACT = mybir.ActivationFunctionType
MULT = mybir.AluOpType.mult
SUB = mybir.AluOpType.subtract

P = 128
PACK = 4
PASS = P * PACK
K, T, E, C, H, N = 128, 1024, 2, 512, 1024, 1024
FLOPS = 2 * E * C * (N * H + 2 * H * K)


def tile_moe_bdx_glu_sigmoid_kernel(
    tc, dyT, a1, a3, w2_words, w2_scales, w1_words, w1_scales, w3_words, w3_scales, gate, offs, out
):
    nc = tc.nc
    with ExitStack() as ctx:
        keep = ctx.enter_context(tc.tile_pool(name="keep", bufs=1))
        ring2 = ctx.enter_context(tc.tile_pool(name="ring2", bufs=2))
        banks = ctx.enter_context(tc.psum_pool(name="banks", bufs=6))
        sums = ctx.enter_context(tc.psum_pool(name="sums", bufs=1))

        offsets = keep.tile([P, E * C // 16], U16, name="offsets")
        gates = keep.tile([P, E * C], F32, name="gates")
        dy = [keep.tile([P, T + 8], F32, name=f"dy{b}") for b in range(N // P)]
        w2_raw = [keep.tile([P, 2 * H], U8, name=f"w2_raw{b}", align_bytes=64) for b in range(4)]
        w2_put = [keep.tile([P, 2 * H], U8, name=f"w2_put{b}", align_bytes=64) for b in range(4)]
        w2s_raw = keep.tile([P, H], U8, name="w2s_raw", align_bytes=64)
        w2s_put = [keep.tile([P, H], U8, name=f"w2s_put{b}", align_bytes=64) for b in range(4)]
        w13 = [keep.tile([P, 4, 2 * K], U8, name=f"w13_{b}", align_bytes=64) for b in range(2)]
        w13s = keep.tile([P, 2, 4, K], U8, name="w13s", align_bytes=64)
        a1_t = [keep.tile([P, PACK, C], F32, name=f"a1_{b}") for b in range(4)]
        a3_t = [keep.tile([P, PACK, C], F32, name=f"a3_{b}") for b in range(4)]
        result = keep.tile([P, T], F32, name="result")

        nc.gpsimd.memset(w2s_raw[:].bitcast(I32), 0)
        for b in range(8):
            nc.gpsimd.memset(dy[b][:, T:], 0.0)
        for b in range(1, 4):
            nc.gpsimd.memset(w2s_put[b][:].bitcast(I32), 0)
        nc.gpsimd.memset(w13s[:].rearrange("p w b k -> p (w b k)").bitcast(I32), 0)

        def load_w2(b):
            nc.sync.dma_start(out=w2_raw[b][:].bitcast(I32), in_=w2_words[b // 2, b % 2].bitcast(I32))

        def load_dy(b):
            s, j = divmod(b, PACK)
            nc.sync.dma_start(out=dy[b][:, 0:T], in_=dyT[s * PASS:(s + 1) * PASS].rearrange("(p j) w -> p j w", j=PACK)[:, j, :])

        for b in range(4):
            load_w2(b)
        nc.sync.dma_start(offsets[:], offs)
        for e in range(E):
            nc.sync.dma_start(out=gates[:, e * C:(e + 1) * C], in_=gate[0:P, e * C:(e + 1) * C])
            load_dy(e)
        for b in range(2, 8):
            load_dy(b)
        for q in range(4):
            nc.scalar.dma_start(
                out=w2s_raw[32 * q:32 * q + 16, :].bitcast(I32),
                in_=w2_scales[:, :, 4 * q:4 * q + 4, :].bitcast(I32).rearrange("e s q i -> (e s) q i"),
            )
        for w, (words, scales) in enumerate(((w1_words, w1_scales), (w3_words, w3_scales))):
            nc.scalar.dma_start(
                out=w13[w][:].rearrange("p b i -> p (b i)").bitcast(I32).rearrange("p (b i) -> p b i", b=4),
                in_=words.bitcast(I32).rearrange("e s p i -> p (e s) i"),
            )
            for q in range(4):
                nc.scalar.dma_start(
                    out=w13s[32 * q:32 * q + 4, w].rearrange("p b i -> p (b i)").bitcast(I32).rearrange("p (b i) -> p b i", b=4),
                    in_=scales[:, :, 4 * q:4 * q + 4, :].bitcast(I32).rearrange("e s q i -> q (e s) i"),
                )
        for b in range(4):
            e, h = divmod(b, 2)
            for src, dst in ((a1, a1_t[b]), (a3, a3_t[b])):
                nc.sync.dma_start(
                    out=dst[:],
                    in_=src[h * PASS:(h + 1) * PASS, e * C:(e + 1) * C].rearrange("(p j) c -> p j c", j=PACK),
                )

        for b in range(4):
            nc.vector.tensor_copy(
                out=w2_put[b][:].bitcast(U16).rearrange("p (h t m) -> p h t m", h=2, t=PACK),
                in_=w2_raw[b][:].bitcast(U16).rearrange("p (h m t) -> p h t m", h=2, t=PACK),
            )
        nc.vector.tensor_copy(
            out=w2s_put[0][:].rearrange("p (h t m) -> p h t m", h=2, t=PACK),
            in_=w2s_raw[:].rearrange("p (h m t) -> p h t m", h=2, t=PACK),
        )
        for b in range(1, 4):
            for q in range(4):
                nc.scalar.dma_start(
                    out=w2s_put[b][32 * q:32 * q + 4, :].bitcast(I32),
                    in_=w2s_put[0][32 * q + 4 * b:32 * q + 4 * b + 4, :].bitcast(I32),
                )

        g_codes, g_scales = {}, {}

        def gather(s, j, g4, first, last):
            slots = slice(first * C, last * C)
            nc.vector.tensor_tensor(
                out=g4[:, j, slots],
                in0=dy[s * PACK + j][:].indirect(offsets[:, first * C // 16:last * C // 16]),
                in1=gates[:, slots],
                op=MULT,
            )

        def interleaved(dst):
            return dst.rearrange("p (c i) t -> p c t i", i=4)

        def planes(src):
            return src.rearrange("p t (c i) -> p c t i", i=4)

        def quantise(src, name):
            codes = keep.tile([P, C], U32, name=name + "_codes", align_bytes=64)
            scales = keep.tile([P, C], U8, name=name + "_scales", align_bytes=64)
            nc.vector.quantize_mx(
                out=codes[:].bitcast(E5M2X4), scales=scales[:], in_=src.rearrange("p c t -> p (c t)")
            )
            return codes, scales

        def finish_g(e, s, g4):
            gb = ring2.tile([P, C, PACK], BF16, name="gb", align_bytes=64)
            nc.scalar.copy(out=interleaved(gb[:]), in_=planes(g4[:, :, e * C:(e + 1) * C]))
            g_codes[e, s], g_scales[e, s] = quantise(gb[:], f"g{e}{s}")

        g4 = [ring2.tile([P, PACK, E * C], F32, name="g4") for s in range(2)]
        gather(0, 0, g4[0], 0, 1)
        gather(0, 0, g4[0], 1, 2)
        for j in range(1, PACK):
            gather(0, j, g4[0], 0, E)
        for e in range(E):
            finish_g(e, 0, g4[0])
        for e in range(E):
            for j in range(PACK):
                gather(1, j, g4[1], e, e + 1)
            finish_g(e, 1, g4[1])

        dx = [sums.tile([P, C], F32, name=f"dx{e}") for e in range(E)]
        held = {}

        def saved(b):
            s = a1_t[b]
            nc.scalar.activation(out=s[:], in_=s[:], func=ACT.Sigmoid)
            v = a3_t[b]
            nc.vector.scalar_tensor_tensor(out=v[:], in0=s[:], scalar=1.0, in1=v[:], op0=SUB, op1=MULT)

        def first_products(b):
            e, h = divmod(b, 2)
            u = ring2.tile([P, PACK, C], F32, name="u")
            for t in range(PACK):
                dh = banks.tile([P, C], F32, name="dh")
                col = h * PASS + t * P
                for s in range(2):
                    nc.tensor.matmul_mx(
                        out=dh[:],
                        lhsT=w2_put[2 * e + s][:, 2 * col:2 * (col + P)].bitcast(E2M1X4),
                        lhsT_scale=w2s_put[2 * e + s][:, col:col + P],
                        rhs=g_codes[e, s][:].bitcast(E5M2X4),
                        rhs_scale=g_scales[e, s][:],
                        start=(s == 0),
                        stop=(s == 1),
                    )
                nc.vector.tensor_tensor(out=u[:, t, :], in0=dh[:], in1=a1_t[b][:, t, :], op=MULT)
            held[b] = u

        def product(engine, b, first, last):
            u, d = held[b]
            engine.tensor_tensor(
                out=interleaved(d[:, 0, first:last, :]),
                in0=planes(u[:, :, first:last]),
                in1=planes(a3_t[b][:, :, first:last]),
                op=MULT,
            )

        def gradients(b, share):
            u = held[b]
            d = ring2.tile([P, 2, C, PACK], BF16, name="d", align_bytes=64)
            held[b] = (u, d)
            for first in range(0, share, 128):
                product(nc.gpsimd, b, first, first + 128)
            nc.scalar.activation(out=interleaved(d[:, 1]), in_=planes(u[:]), func=ACT.Copy, scale=-1.0)

        def second_products(b):
            e, h = divmod(b, 2)
            for w in range(2):
                codes, scales = quantise(held[b][1][:, w], f"d{w}_{b}")
                nc.tensor.matmul_mx(
                    out=dx[e][:],
                    lhsT=w13[w][:, b, :].bitcast(E2M1X4),
                    lhsT_scale=w13s[:, w, b, :],
                    rhs=codes[:].bitcast(E5M2X4),
                    rhs_scale=scales[:],
                    start=(h == 0 and w == 0),
                    stop=(h == 1 and w == 1),
                )

        def finish(e, dx_sb):
            nc.scalar.activation(out=dx_sb[:, 0, :], in_=dx[e][:], func=ACT.Copy, scale=-1.0)

        def scatter(e, dx_sb):
            nc.vector.tensor_copy(result[:].indirect(offsets[:, e * C // 16:(e + 1) * C // 16]), dx_sb[:, 0, :])

        saved(0)
        first_products(0)
        saved(1)
        for b in range(4):
            share = 256 if b < 3 else 0
            gradients(b, share)
            if b < 3:
                first_products(b + 1)
            product(nc.vector, b, share, C)
            if b < 2:
                saved(b + 2)
            second_products(b)
        landing = [ring2.tile([P, PACK, C], F32, name="u") for z in range(2)]
        for e in range(E):
            finish(e, landing[1 - e])
            scatter(e, landing[1 - e])
        nc.sync.dma_start(out=out, in_=result[:])
